import numpy as np
import ml_dtypes


def mxq(x, axis, fmt="e4m3"):
    dtype, down = {"e4m3": (ml_dtypes.float8_e4m3fn, 7), "e5m2": (ml_dtypes.float8_e5m2, 14)}[fmt]
    v = np.moveaxis(np.asarray(x, np.float32).astype(ml_dtypes.bfloat16).astype(np.float64), axis, -1)
    blocks = v.reshape(v.shape[:-1] + (-1, 32))
    amax = np.abs(blocks).max(-1, keepdims=True)
    byte = np.maximum(np.where(amax > 0, np.frexp(amax)[1] - 1 + 127, 0) - down, 1)
    scale = np.exp2(byte - 127.0)
    codes = (blocks / scale).astype(np.float32).astype(dtype).astype(np.float64)
    return np.moveaxis((codes * scale).reshape(v.shape), -1, axis)


WIDE = False


def mx_kscale(k):
    if not WIDE:
        return np.ones(k)
    levels = np.array([10, -10, 5, -5, 0])
    if k % 512:
        return np.exp2(np.random.permutation(np.resize(levels, k // 32))).repeat(32)
    a = np.empty((k // 512, 16))
    for p in range(k // 512):
        a[p, :8] = np.random.permutation(np.resize(levels, 8))
        for g in range(8):
            far = levels[np.abs(levels - a[p, g]) >= 10]
            a[p, g + 8] = far[np.random.randint(len(far))]
    return np.exp2(a.ravel()).repeat(32)


def f64(x):
    return np.asarray(x).astype(np.float64)


def striped(idx):
    return np.tile(idx.reshape(-1, 16).T, (8, 1)).astype(np.uint16)


def unstriped(offs):
    return offs[:16].T.reshape(-1).astype(np.int64)


def silu(v):
    return v / (1.0 + np.exp(-np.maximum(v, -700.0)))


K, T, E, C, H, N = 512, 512, 4, 256, 512, 128


def by_expert(wq, xq):
    return np.concatenate([wq[e].T @ xq[:, e * C:(e + 1) * C] for e in range(E)], axis=1)


def setup_inputs():
    n = np.random.standard_normal
    s = mx_kscale(K)[:, None]
    u = mx_kscale(H)
    first = np.random.permutation(np.repeat(np.arange(E), T // E))
    second = (first + 1 + np.random.permutation(np.repeat(np.arange(E - 1), -(-T // (E - 1)))[:T])) % E
    while np.bincount(second, minlength=E).max() != T // E:
        load = np.bincount(second, minlength=E); hi, lo = int(load.argmax()), int(load.argmin())
        t = np.flatnonzero((second == hi) & (first != lo))[0]; second[t] = lo
    slot_token = np.empty(E * C, np.int64); pos = np.empty((2, T), np.int64); fill = np.zeros(E, np.int64)
    place = np.stack([np.random.permutation(C) for _ in range(E)])
    for r, deal in enumerate((first, second)):
        for t in np.random.permutation(T):
            e = deal[t]; j = e * C + place[e, fill[e]]; fill[e] += 1; slot_token[j] = t; pos[r, t] = j
    g = np.random.uniform(0.2, 0.8, T)
    return {
        "xT": (n((K, T)) * s).astype(np.float32),
        "w1": (n((E, K, H)) / np.sqrt(K) / s[None] * u[None, None, :]).astype(np.float32),
        "w2": (n((E, H, N)) / np.sqrt(H) / u[None, :, None]).astype(np.float32),
        "gate": np.stack([np.tile(g, (N, 1)), np.tile(1.0 - g, (N, 1))]).astype(np.float32),
        "offs": striped(slot_token),
        "pos1": striped(pos[0]),
        "pos2": striped(pos[1]),
    }


def reference(xT, w1, w2, gate, offs, pos1, pos2):
    idx = unstriped(offs)
    xq = mxq(f64(xT)[:, idx], 0, "e4m3")
    h = silu(by_expert(mxq(f64(w1), 1, "e4m3"), xq))
    y = by_expert(mxq(f64(w2), 1, "e4m3"), mxq(h, 0, "e4m3"))
    return f64(gate[0]) * y[:, unstriped(pos1)] + f64(gate[1]) * y[:, unstriped(pos2)]

@@ -1,0 +1,199 @@
+from contextlib import ExitStack
+
+import concourse.mybir as mybir
+
+K, T, E, C, H, N = 512, 512, 4, 256, 512, 128
+FLOPS = 2 * E * C * (K * H + H * N)
+
+F32 = mybir.dt.float32
+BF16 = mybir.dt.bfloat16
+U32 = mybir.dt.uint32
+U16 = mybir.dt.uint16
+U8 = mybir.dt.uint8
+FP8X4 = mybir.dt.float8_e4m3fn_x4
+ACT = mybir.ActivationFunctionType
+ALU = mybir.AluOpType
+P = 128
+UNIT = 128
+
+XV = [48,40]
+CUTS = [[0,24],[24,40],[40,64]]
+W1V = [0,80,0,48]
+W1G = [48,48,16,64]
+W2ENG = ["G","G","V","G"]
+HQ = [1,2,1,1]
+YC = [["S",1],["V",2],["V",1],["S",1]]
+DMA = "xa offs xb w12 w10 w13 p2 w11 p1 w2b w2a gate"
+STEPS = "xv0 xs0 qx0 xs1 xv1 qx1 gw1 gb2 is2 ig2 gb1 gb0 is0 ig0 gw0 q12 q10 mm20 is3 ig3 iv3 mm00 silu20 mm01 gw2 silu00 q13 mm21 silu01 ig1 iv1 mm31 silu21 mm30 qh00 q11 silu31 i23 i22 mm11 silu30 qh20 mm10 i20 q22 silu11 qh30 y20 i21 q20 y30 silu10 yc2 y00 qh11 q21 yc0 qh10 y11 yc11 y10 yc3 yc10 z1 z0 add"
+
+
+def tile_routed_moe_kernel(tc, xT, w1, w2, gate, offs, pos1, pos2, out):
+    nc = tc.nc
+    with ExitStack() as ctx:
+        keep = ctx.enter_context(tc.tile_pool(name="keep", bufs=1))
+        banks = ctx.enter_context(tc.psum_pool(name="banks", bufs=4))
+
+        def mk(shape, dt, name):
+            return keep.tile(shape, dt, name=name, align_bytes=64)
+
+        offs_sb = keep.tile([P, E * C // 16], U16, name="offs_sb")
+        pos1_sb = keep.tile([P, T // 16], U16, name="pos1_sb")
+        pos2_sb = keep.tile([P, T // 16], U16, name="pos2_sb")
+        warm = mk([P, 2], F32, "warm")
+        nc.vector.memset(warm[:, 0:1], 0.0)
+        nc.scalar.activation(warm[:, 1:2], warm[:, 0:1], ACT.Silu)
+
+        x_raw = [mk([P, 4, T // 2], F32, f"x_raw{a}") for a in range(2)]
+        w1_raw = [mk([P, 4, H], F32, f"w1_raw{e}") for e in range(E)]
+        w2_raw = mk([P, E, 4, N], F32, "w2_raw")
+        gate_sb = mk([P, 2, T], F32, "gate_sb")
+        x_src = xT.rearrange("(p j) t -> p j t", j=4)
+        w1_src = w1.rearrange("e (p j) c -> e p j c", j=4)
+        w2_src = w2.rearrange("e (p j) n -> p e j n", j=4)
+        for d in DMA.split(" "):
+            if d == "offs":
+                nc.sync.dma_start(offs_sb[:], offs)
+            elif d == "p1":
+                nc.sync.dma_start(pos1_sb[:], pos1)
+            elif d == "p2":
+                nc.sync.dma_start(pos2_sb[:], pos2)
+            elif d == "gate":
+                nc.sync.dma_start(gate_sb[:], gate.rearrange("g p t -> p g t"))
+            elif d == "xa":
+                nc.sync.dma_start(x_raw[0][:], x_src[:, :, 0:256])
+            elif d == "xb":
+                nc.sync.dma_start(x_raw[1][:], x_src[:, :, 256:512])
+            elif d == "w2a":
+                nc.sync.dma_start(w2_raw[:, 0:1], w2_src[:, 0:1])
+            elif d == "w2b":
+                nc.sync.dma_start(w2_raw[:, 1:4], w2_src[:, 1:4])
+            else:
+                e = int(d[2])
+                nc.sync.dma_start(w1_raw[e][:], w1_src[e])
+
+        x_words = mk([P, T], U32, "x_words")
+        x_bytes = mk([P, T], U8, "x_bytes")
+        nc.gpsimd.memset(x_bytes[:], 0)
+        x_grouped = [mk([P, 1024], BF16, f"x_grouped{a}") for a in range(2)]
+        g_words = [mk([P, 16 * (b - a)], U32, f"g_words{a}") for a, b in CUTS]
+        g_bytes = [mk([P, 16 * (b - a)], U8, f"g_bytes{a}") for a, b in CUTS]
+        w1_grouped = [mk([P, 4 * H], BF16, f"w1_grouped{e}") for e in range(E)]
+        w1_words = [mk([P, H], U32, f"w1_words{e}") for e in range(E)]
+        w1_bytes = [mk([P, H], U8, f"w1_bytes{e}") for e in range(E)]
+        w2_grouped = mk([P, E * 4 * N], BF16, "w2_grouped")
+        w2_words = mk([P, E * N], U32, "w2_words")
+        w2_bytes = mk([P, E * N], U8, "w2_bytes")
+        h_grouped = [mk([P, 2, UNIT, 4], BF16, f"h_grouped{e}") for e in range(E)]
+        h_words = [mk([P, 2 * UNIT], U32, f"h_words{e}") for e in range(E)]
+        h_bytes = [mk([P, 2 * UNIT], U8, f"h_bytes{e}") for e in range(E)]
+        y_all = mk([P, E * C], F32, "y_all")
+        z = [mk([P, T], F32, f"z{r}") for r in range(2)]
+        res = mk([P, T], F32, "res")
+        a_ps = {}
+        y_ps = {}
+
+        def copy(eng, dst, src):
+            if eng == "v":
+                nc.vector.tensor_copy(dst, src)
+            elif eng == "s":
+                nc.scalar.copy(dst, src)
+            else:
+                nc.gpsimd.tensor_scalar(dst, src, 1.0, 0.0, ALU.mult, ALU.add)
+
+        def quantize(words, byts, src):
+            nc.vector.quantize_mx(out=words.bitcast(FP8X4), scales=byts, in_=src)
+
+        def step(n):
+            if n[0] == "x":
+                a = int(n[2])
+                dst = x_grouped[a][:].rearrange("p (c i j) -> p c j i", i=4, j=4)
+                src = x_raw[a][:].rearrange("p j (c i) -> p c j i", i=4)
+                r = slice(0, XV[a]) if n[1] == "v" else slice(XV[a], 64)
+                copy(n[1], dst[:, r], src[:, r])
+            elif n.startswith("qx"):
+                a = int(n[2])
+                r = slice(256 * a, 256 * a + 256)
+                quantize(x_words[:, r], x_bytes[:, r], x_grouped[a][:])
+            elif n[0] == "g":
+                k = int(n[2])
+                o = offs_sb[:, CUTS[k][0] : CUTS[k][1]]
+                if n[1] == "w":
+                    nc.vector.tensor_copy(g_words[k][:], x_words[:].indirect(o))
+                else:
+                    nc.vector.tensor_copy(g_bytes[k][:], x_bytes[:].indirect(o))
+            elif n.startswith("i2"):
+                e = int(n[2])
+                copy(
+                    {"V": "v", "S": "s", "G": "g"}[W2ENG[e]],
+                    w2_grouped[:, e * 512 : e * 512 + 512].rearrange("p (c i j) -> p c j i", i=4, j=4),
+                    w2_raw[:, e].rearrange("p j (c i) -> p c j i", i=4),
+                )
+            elif n[0] == "i":
+                e = int(n[2])
+                dst = w1_grouped[e][:].rearrange("p (t m j) -> p m j t", t=4, j=4)
+                src = w1_raw[e][:].rearrange("p j (m t) -> p m j t", t=4)
+                r = {"v": slice(0, W1V[e]), "g": slice(W1V[e], W1V[e] + W1G[e]), "s": slice(W1V[e] + W1G[e], P)}[n[1]]
+                copy(n[1], dst[:, r], src[:, r])
+            elif n.startswith("q1"):
+                e = int(n[2])
+                quantize(w1_words[e][:], w1_bytes[e][:], w1_grouped[e][:])
+            elif n.startswith("q2"):
+                e = int(n[2])
+                f = 4 if e == 2 else e + 1
+                quantize(w2_words[:, e * N : f * N], w2_bytes[:, e * N : f * N], w2_grouped[:, e * 512 : f * 512])
+            elif n.startswith("mm"):
+                e, u = int(n[2]), int(n[3])
+                bank = banks.tile([P, 4, UNIT], F32, name="a_ps")
+                a_ps[e, u] = bank
+                col = e * 16 + u * 8
+                for k, ab in enumerate(CUTS):
+                    if ab[0] <= col < ab[1]:
+                        s = slice((col - ab[0]) * 16, (col - ab[0]) * 16 + UNIT)
+                        for t in range(4):
+                            m = slice(t * P, (t + 1) * P)
+                            nc.tensor.matmul_mx(
+                                out=bank[:, t, :],
+                                lhsT=w1_words[e][:, m].bitcast(FP8X4), lhsT_scale=w1_bytes[e][:, m],
+                                rhs=g_words[k][:, s].bitcast(FP8X4), rhs_scale=g_bytes[k][:, s],
+                                start=True, stop=True,
+                            )
+            elif n.startswith("silu"):
+                e, u = int(n[4]), int(n[5])
+                nc.scalar.activation(h_grouped[e][:, u], a_ps[e, u][:].rearrange("p t n -> p n t"), ACT.Silu)
+            elif n.startswith("qh"):
+                e, u = int(n[2]), int(n[3])
+                r = slice(u * UNIT, (u + 1) * UNIT) if HQ[e] == 2 else slice(0, 2 * UNIT)
+                g = h_grouped[e][:].rearrange("p u n t -> p (u n t)")
+                quantize(h_words[e][:, r], h_bytes[e][:, r], g[:, r.start * 4 : r.stop * 4])
+            elif n.startswith("yc"):
+                e = int(n[2])
+                if YC[e][1] == 1:
+                    copy("v" if YC[e][0] == "V" else "s", y_all[:, e * C : e * C + C], y_ps[e][:])
+                else:
+                    u = int(n[3])
+                    g = YC[e][0][u] if len(YC[e][0]) == 2 else YC[e][0]
+                    copy("v" if g == "V" else "s", y_all[:, e * C + u * UNIT : e * C + (u + 1) * UNIT], y_ps[e][:, u * UNIT : (u + 1) * UNIT])
+            elif n[0] == "y":
+                e, u = int(n[1]), int(n[2])
+                if e not in y_ps:
+                    bank = banks.tile([P, 2 * UNIT], F32, name="y_ps")
+                    y_ps[e] = bank
+                r = slice(u * UNIT, (u + 1) * UNIT) if HQ[e] == 2 else slice(0, 2 * UNIT)
+                w = slice(e * N, (e + 1) * N)
+                nc.tensor.matmul_mx(
+                    out=y_ps[e][:, r],
+                    lhsT=w2_words[:, w].bitcast(FP8X4), lhsT_scale=w2_bytes[:, w],
+                    rhs=h_words[e][:, r].bitcast(FP8X4), rhs_scale=h_bytes[e][:, r],
+                    start=True, stop=True,
+                )
+            elif n[0] == "z":
+                r = int(n[1])
+                nc.vector.tensor_tensor(z[r][:], y_all[:].indirect((pos1_sb, pos2_sb)[r][:]), gate_sb[:, r, :], ALU.mult)
+            elif n == "add":
+                for a in range(2):
+                    r = slice(a * 256, (a + 1) * 256)
+                    nc.vector.tensor_tensor(res[:, r], z[0][:, r], z[1][:, r], ALU.add)
+                    (nc.sync, nc.scalar)[a].dma_start(out[:, r], res[:, r])
+
+        for n in STEPS.split(" "):
+            step(n)

@@ -16,15 +16,15 @@ ALU = mybir.AluOpType
 P = 128
 UNIT = 128
 
-XV = [48,40]
-CUTS = [[0,24],[24,40],[40,64]]
-W1V = [0,80,0,48]
-W1G = [48,48,16,64]
-W2ENG = ["G","G","V","G"]
-HQ = [1,2,1,1]
-YC = [["S",1],["V",2],["V",1],["S",1]]
-DMA = "xa offs xb w12 w10 w13 p2 w11 p1 w2b w2a gate"
-STEPS = "xv0 xs0 qx0 xs1 xv1 qx1 gw1 gb2 is2 ig2 gb1 gb0 is0 ig0 gw0 q12 q10 mm20 is3 ig3 iv3 mm00 silu20 mm01 gw2 silu00 q13 mm21 silu01 ig1 iv1 mm31 silu21 mm30 qh00 q11 silu31 i23 i22 mm11 silu30 qh20 mm10 i20 q22 silu11 qh30 y20 i21 q20 y30 silu10 yc2 y00 qh11 q21 yc0 qh10 y11 yc11 y10 yc3 yc10 z1 z0 add"
+XV = [48,48]
+CUTS = [[0,24],[24,48],[48,64]]
+W1V = [0,0,112,112]
+W1G = [0,0,0,0]
+W2ENG = ["S","V","V","V"]
+HQ = [1,1,1,2]
+YC = [["V",1],["S",1],["S",1],["V",2]]
+DMA = "xa xb offs w2a w11 p1 w10 p2 w12 w13 w2b gate"
+STEPS = "xv0 xs0 qx0 xv1 xs1 i20 qx1 gb2 gw2 gw0 is1 gb0 q20 gb1 is0 q11 gw1 mm10 iv2 mm11 is2 silu11 q10 silu10 q12 mm00 mm01 silu00 iv3 mm21 mm20 is3 qh10 silu01 q13 silu20 i23 mm30 qh00 mm31 silu30 i21 y00 i22 silu21 yc0 q22 silu31 q21 qh20 y10 qh30 yc1 y20 qh31 y30 yc30 y31 yc2 yc31 z0 z1 add"
 
 
 def tile_routed_moe_kernel(tc, xT, w1, w2, gate, offs, pos1, pos2, out):

@@ -16,15 +16,16 @@ ALU = mybir.AluOpType
 P = 128
 UNIT = 128
 
-XV = [48,48]
-CUTS = [[0,24],[24,48],[48,64]]
-W1V = [0,0,112,112]
+XV = [16,64]
+CUTS = [[0,16],[16,40],[40,64]]
+W1V = [32,48,0,112]
 W1G = [0,0,0,0]
-W2ENG = ["S","V","V","V"]
+W2ENG = ["V","V","S","V"]
+Q2 = 2
 HQ = [1,1,1,2]
-YC = [["V",1],["S",1],["S",1],["V",2]]
-DMA = "xa xb offs w2a w11 p1 w10 p2 w12 w13 w2b gate"
-STEPS = "xv0 xs0 qx0 xv1 xs1 i20 qx1 gb2 gw2 gw0 is1 gb0 q20 gb1 is0 q11 gw1 mm10 iv2 mm11 is2 silu11 q10 silu10 q12 mm00 mm01 silu00 iv3 mm21 mm20 is3 qh10 silu01 q13 silu20 i23 mm30 qh00 mm31 silu30 i21 y00 i22 silu21 yc0 q22 silu31 q21 qh20 y10 qh30 yc1 y20 qh31 y30 yc30 y31 yc2 yc31 z0 z1 add"
+YC = [["S",1],["S",1],["V",1],["VS",2]]
+DMA = "offs x w12 w10 w11 w13 w2b w2a p2 p1 gate"
+STEPS = "xv1 xs0 xv0 qx1 qx0 gb0 is2 gw0 gw2 gb2 is0 q12 gb1 mm21 is1 iv0 gw1 silu21 q10 mm20 is3 iv1 mm01 silu20 iv3 mm00 silu01 q11 i22 q13 mm11 silu00 i21 mm10 i20 silu11 mm30 qh20 qh00 mm31 silu10 q20 i23 y00 silu30 qh10 q22 silu31 y10 qh30 y20 yc1 y30 qh31 yc2 yc0 y31 yc30 yc31 z0 z1a adda z1b add"
 
 
 def tile_routed_moe_kernel(tc, xT, w1, w2, gate, offs, pos1, pos2, out):
@@ -43,7 +44,7 @@ def tile_routed_moe_kernel(tc, xT, w1, w2, gate, offs, pos1, pos2, out):
         nc.vector.memset(warm[:, 0:1], 0.0)
         nc.scalar.activation(warm[:, 1:2], warm[:, 0:1], ACT.Silu)
 
-        x_raw = [mk([P, 4, T // 2], F32, f"x_raw{a}") for a in range(2)]
+        x_raw = mk([P, 4, T], F32, "x_raw")
         w1_raw = [mk([P, 4, H], F32, f"w1_raw{e}") for e in range(E)]
         w2_raw = mk([P, E, 4, N], F32, "w2_raw")
         gate_sb = mk([P, 2, T], F32, "gate_sb")
@@ -59,14 +60,16 @@ def tile_routed_moe_kernel(tc, xT, w1, w2, gate, offs, pos1, pos2, out):
                 nc.sync.dma_start(pos2_sb[:], pos2)
             elif d == "gate":
                 nc.sync.dma_start(gate_sb[:], gate.rearrange("g p t -> p g t"))
+            elif d == "x":
+                nc.sync.dma_start(x_raw[:], x_src)
             elif d == "xa":
-                nc.sync.dma_start(x_raw[0][:], x_src[:, :, 0:256])
+                nc.sync.dma_start(x_raw[:, :, 0:256], x_src[:, :, 0:256])
             elif d == "xb":
-                nc.sync.dma_start(x_raw[1][:], x_src[:, :, 256:512])
+                nc.sync.dma_start(x_raw[:, :, 256:512], x_src[:, :, 256:512])
             elif d == "w2a":
-                nc.sync.dma_start(w2_raw[:, 0:1], w2_src[:, 0:1])
+                nc.sync.dma_start(w2_raw[:, 0:2], w2_src[:, 0:2])
             elif d == "w2b":
-                nc.sync.dma_start(w2_raw[:, 1:4], w2_src[:, 1:4])
+                nc.sync.dma_start(w2_raw[:, 2:4], w2_src[:, 2:4])
             else:
                 e = int(d[2])
                 nc.sync.dma_start(w1_raw[e][:], w1_src[e])
@@ -107,7 +110,7 @@ def tile_routed_moe_kernel(tc, xT, w1, w2, gate, offs, pos1, pos2, out):
             if n[0] == "x":
                 a = int(n[2])
                 dst = x_grouped[a][:].rearrange("p (c i j) -> p c j i", i=4, j=4)
-                src = x_raw[a][:].rearrange("p j (c i) -> p c j i", i=4)
+                src = x_raw[:, :, 256 * a : 256 * a + 256].rearrange("p j (c i) -> p c j i", i=4)
                 r = slice(0, XV[a]) if n[1] == "v" else slice(XV[a], 64)
                 copy(n[1], dst[:, r], src[:, r])
             elif n.startswith("qx"):
@@ -123,23 +126,33 @@ def tile_routed_moe_kernel(tc, xT, w1, w2, gate, offs, pos1, pos2, out):
                     nc.vector.tensor_copy(g_bytes[k][:], x_bytes[:].indirect(o))
             elif n.startswith("i2"):
                 e = int(n[2])
-                copy(
-                    {"V": "v", "S": "s", "G": "g"}[W2ENG[e]],
-                    w2_grouped[:, e * 512 : e * 512 + 512].rearrange("p (c i j) -> p c j i", i=4, j=4),
-                    w2_raw[:, e].rearrange("p j (c i) -> p c j i", i=4),
-                )
+                dst = w2_grouped[:, e * 512 : e * 512 + 512]
+                if W2ENG[e] == "G":
+                    copy("g", dst.rearrange("p (c j) -> p c j", j=4), w2_raw[:, e].rearrange("p j c -> p c j"))
+                else:
+                    copy(
+                        {"V": "v", "S": "s"}[W2ENG[e]],
+                        dst.rearrange("p (c i j) -> p c j i", i=4, j=4),
+                        w2_raw[:, e].rearrange("p j (c i) -> p c j i", i=4),
+                    )
             elif n[0] == "i":
                 e = int(n[2])
                 dst = w1_grouped[e][:].rearrange("p (t m j) -> p m j t", t=4, j=4)
                 src = w1_raw[e][:].rearrange("p j (m t) -> p m j t", t=4)
                 r = {"v": slice(0, W1V[e]), "g": slice(W1V[e], W1V[e] + W1G[e]), "s": slice(W1V[e] + W1G[e], P)}[n[1]]
-                copy(n[1], dst[:, r], src[:, r])
+                if n[1] == "g":
+                    dst = w1_grouped[e][:].rearrange("p (t m j) -> p t m j", t=4, j=4)
+                    src = w1_raw[e][:].rearrange("p j (m t) -> p t m j", t=4)
+                    for t in range(4):
+                        copy("g", dst[:, t, r], src[:, t, r])
+                else:
+                    copy(n[1], dst[:, r], src[:, r])
             elif n.startswith("q1"):
                 e = int(n[2])
                 quantize(w1_words[e][:], w1_bytes[e][:], w1_grouped[e][:])
             elif n.startswith("q2"):
                 e = int(n[2])
-                f = 4 if e == 2 else e + 1
+                f = 4 if (e == 2 or Q2 == 1) else 2
                 quantize(w2_words[:, e * N : f * N], w2_bytes[:, e * N : f * N], w2_grouped[:, e * 512 : f * 512])
             elif n.startswith("mm"):
                 e, u = int(n[2]), int(n[3])
@@ -186,14 +199,17 @@ def tile_routed_moe_kernel(tc, xT, w1, w2, gate, offs, pos1, pos2, out):
                     rhs=h_words[e][:, r].bitcast(FP8X4), rhs_scale=h_bytes[e][:, r],
                     start=True, stop=True,
                 )
+            elif n == "z0":
+                nc.vector.tensor_tensor(z[0][:], y_all[:].indirect(pos1_sb[:]), gate_sb[:, 0, :], ALU.mult)
             elif n[0] == "z":
-                r = int(n[1])
-                nc.vector.tensor_tensor(z[r][:], y_all[:].indirect((pos1_sb, pos2_sb)[r][:]), gate_sb[:, r, :], ALU.mult)
-            elif n == "add":
-                for a in range(2):
-                    r = slice(a * 256, (a + 1) * 256)
-                    nc.vector.tensor_tensor(res[:, r], z[0][:, r], z[1][:, r], ALU.add)
-                    (nc.sync, nc.scalar)[a].dma_start(out[:, r], res[:, r])
+                a = 0 if n == "z1a" else 1
+                r = slice(a * 256, (a + 1) * 256)
+                nc.vector.tensor_tensor(z[1][:, r], y_all[:].indirect(pos2_sb[:, 16 * a : 16 * a + 16]), gate_sb[:, 1, r], ALU.mult)
+            else:
+                a = 0 if n == "adda" else 1
+                r = slice(a * 256, (a + 1) * 256)
+                nc.vector.tensor_tensor(res[:, r], z[0][:, r], z[1][:, r], ALU.add)
+                (nc.sync, nc.scalar)[a].dma_start(out[:, r], res[:, r])
 
         for n in STEPS.split(" "):
             step(n)

@@ -12,204 +12,192 @@ U16 = mybir.dt.uint16
 U8 = mybir.dt.uint8
 FP8X4 = mybir.dt.float8_e4m3fn_x4
 ACT = mybir.ActivationFunctionType
-ALU = mybir.AluOpType
-P = 128
-UNIT = 128
+MULT, ADD = mybir.AluOpType.mult, mybir.AluOpType.add
 
-XV = [16,64]
-CUTS = [[0,16],[16,40],[40,64]]
-W1V = [32,48,0,112]
-W1G = [0,0,0,0]
-W2ENG = ["V","V","S","V"]
-Q2 = 2
-HQ = [1,1,1,2]
-YC = [["S",1],["S",1],["V",1],["VS",2]]
-DMA = "offs x w12 w10 w11 w13 w2b w2a p2 p1 gate"
-STEPS = "xv1 xs0 xv0 qx1 qx0 gb0 is2 gw0 gw2 gb2 is0 q12 gb1 mm21 is1 iv0 gw1 silu21 q10 mm20 is3 iv1 mm01 silu20 iv3 mm00 silu01 q11 i22 q13 mm11 silu00 i21 mm10 i20 silu11 mm30 qh20 qh00 mm31 silu10 q20 i23 y00 silu30 qh10 q22 silu31 y10 qh30 y20 yc1 y30 qh31 yc2 yc0 y31 yc30 yc31 z0 z1a adda z1b add"
+P = 128
+PACK = 4
+HALF_T = T // 2
+UNIT = 128
+UNITS = C // UNIT
+LANE = 16
+
+GATHERS = ((0, 384), (384, 768), (768, 1024))
+X_VECTOR_GROUPS = 48
+W1_VECTOR_COLUMNS = (0, 0, 96, 96)
 
 
 def tile_routed_moe_kernel(tc, xT, w1, w2, gate, offs, pos1, pos2, out):
     nc = tc.nc
     with ExitStack() as ctx:
+        lists = ctx.enter_context(tc.tile_pool(name="lists", bufs=1))
         keep = ctx.enter_context(tc.tile_pool(name="keep", bufs=1))
         banks = ctx.enter_context(tc.psum_pool(name="banks", bufs=4))
 
-        def mk(shape, dt, name):
-            return keep.tile(shape, dt, name=name, align_bytes=64)
+        def tile(shape, dtype, name):
+            return keep.tile(shape, dtype, name=name, align_bytes=64)
 
-        offs_sb = keep.tile([P, E * C // 16], U16, name="offs_sb")
-        pos1_sb = keep.tile([P, T // 16], U16, name="pos1_sb")
-        pos2_sb = keep.tile([P, T // 16], U16, name="pos2_sb")
-        warm = mk([P, 2], F32, "warm")
-        nc.vector.memset(warm[:, 0:1], 0.0)
-        nc.scalar.activation(warm[:, 1:2], warm[:, 0:1], ACT.Silu)
+        table = tile([P, 2], F32, "table")
+        nc.vector.memset(table[:, 0:1], 0.0)
+        nc.scalar.activation(table[:, 1:2], table[:, 0:1], ACT.Silu)
 
-        x_raw = mk([P, 4, T], F32, "x_raw")
-        w1_raw = [mk([P, 4, H], F32, f"w1_raw{e}") for e in range(E)]
-        w2_raw = mk([P, E, 4, N], F32, "w2_raw")
-        gate_sb = mk([P, 2, T], F32, "gate_sb")
-        x_src = xT.rearrange("(p j) t -> p j t", j=4)
-        w1_src = w1.rearrange("e (p j) c -> e p j c", j=4)
-        w2_src = w2.rearrange("e (p j) n -> p e j n", j=4)
-        for d in DMA.split(" "):
-            if d == "offs":
-                nc.sync.dma_start(offs_sb[:], offs)
-            elif d == "p1":
-                nc.sync.dma_start(pos1_sb[:], pos1)
-            elif d == "p2":
-                nc.sync.dma_start(pos2_sb[:], pos2)
-            elif d == "gate":
-                nc.sync.dma_start(gate_sb[:], gate.rearrange("g p t -> p g t"))
-            elif d == "x":
-                nc.sync.dma_start(x_raw[:], x_src)
-            elif d == "xa":
-                nc.sync.dma_start(x_raw[:, :, 0:256], x_src[:, :, 0:256])
-            elif d == "xb":
-                nc.sync.dma_start(x_raw[:, :, 256:512], x_src[:, :, 256:512])
-            elif d == "w2a":
-                nc.sync.dma_start(w2_raw[:, 0:2], w2_src[:, 0:2])
-            elif d == "w2b":
-                nc.sync.dma_start(w2_raw[:, 2:4], w2_src[:, 2:4])
-            else:
-                e = int(d[2])
-                nc.sync.dma_start(w1_raw[e][:], w1_src[e])
+        offs_sb = lists.tile([P, E * C // LANE], U16, name="offs_sb")
+        pos1_sb = lists.tile([P, T // LANE], U16, name="pos1_sb")
+        pos2_sb = lists.tile([P, T // LANE], U16, name="pos2_sb")
+        x_raw = [tile([P, PACK, HALF_T], F32, f"x_raw{a}") for a in range(2)]
+        w1_raw = [tile([P, PACK, H], F32, f"w1_raw{e}") for e in range(E)]
+        w2_raw = [tile([P, 2, PACK, N], F32, f"w2_raw{b}") for b in range(2)]
+        gate_sb = tile([P, 2, T], F32, "gate_sb")
 
-        x_words = mk([P, T], U32, "x_words")
-        x_bytes = mk([P, T], U8, "x_bytes")
+        x_rows = xT.rearrange("(p j) t -> p j t", j=PACK)
+        w1_rows = w1.rearrange("e (p j) i -> e p j i", j=PACK)
+        w2_rows = w2.rearrange("e (p j) n -> p e j n", j=PACK)
+        nc.sync.dma_start(offs_sb[:], offs)
+        for a in range(2):
+            nc.sync.dma_start(x_raw[a][:], x_rows[:, :, a * HALF_T : (a + 1) * HALF_T])
+        for e in range(E):
+            nc.sync.dma_start(w1_raw[e][:], w1_rows[e])
+        for b in range(2):
+            nc.sync.dma_start(w2_raw[b][:], w2_rows[:, 2 * b : 2 * b + 2])
+        nc.sync.dma_start(pos1_sb[:], pos1)
+        nc.sync.dma_start(pos2_sb[:], pos2)
+        nc.sync.dma_start(gate_sb[:], gate.rearrange("g p t -> p g t"))
+
+        x_grouped = [tile([P, HALF_T * PACK], BF16, f"x_grouped{a}") for a in range(2)]
+        x_words = tile([P, T], U32, "x_words")
+        x_bytes = tile([P, T], U8, "x_bytes")
+        g_words = [tile([P, hi - lo], U32, f"g_words{lo}") for lo, hi in GATHERS]
+        g_bytes = [tile([P, hi - lo], U8, f"g_bytes{lo}") for lo, hi in GATHERS]
+        w1_grouped = [tile([P, H * PACK], BF16, f"w1_grouped{e}") for e in range(E)]
+        w1_words = [tile([P, H], U32, f"w1_words{e}") for e in range(E)]
+        w1_bytes = [tile([P, H], U8, f"w1_bytes{e}") for e in range(E)]
+        w2_grouped = [tile([P, 2 * N * PACK], BF16, f"w2_grouped{b}") for b in range(2)]
+        w2_words = [tile([P, 2 * N], U32, f"w2_words{b}") for b in range(2)]
+        w2_bytes = [tile([P, 2 * N], U8, f"w2_bytes{b}") for b in range(2)]
+        h_grouped = [tile([P, C, PACK], BF16, f"h_grouped{e}") for e in range(E)]
+        h_words = [tile([P, C], U32, f"h_words{e}") for e in range(E)]
+        h_bytes = [tile([P, C], U8, f"h_bytes{e}") for e in range(E)]
+        y_all = tile([P, E * C], F32, "y_all")
+        z = [tile([P, T], F32, f"z{r}") for r in range(2)]
+        total = tile([P, T], F32, "total")
+
         nc.gpsimd.memset(x_bytes[:], 0)
-        x_grouped = [mk([P, 1024], BF16, f"x_grouped{a}") for a in range(2)]
-        g_words = [mk([P, 16 * (b - a)], U32, f"g_words{a}") for a, b in CUTS]
-        g_bytes = [mk([P, 16 * (b - a)], U8, f"g_bytes{a}") for a, b in CUTS]
-        w1_grouped = [mk([P, 4 * H], BF16, f"w1_grouped{e}") for e in range(E)]
-        w1_words = [mk([P, H], U32, f"w1_words{e}") for e in range(E)]
-        w1_bytes = [mk([P, H], U8, f"w1_bytes{e}") for e in range(E)]
-        w2_grouped = mk([P, E * 4 * N], BF16, "w2_grouped")
-        w2_words = mk([P, E * N], U32, "w2_words")
-        w2_bytes = mk([P, E * N], U8, "w2_bytes")
-        h_grouped = [mk([P, 2, UNIT, 4], BF16, f"h_grouped{e}") for e in range(E)]
-        h_words = [mk([P, 2 * UNIT], U32, f"h_words{e}") for e in range(E)]
-        h_bytes = [mk([P, 2 * UNIT], U8, f"h_bytes{e}") for e in range(E)]
-        y_all = mk([P, E * C], F32, "y_all")
-        z = [mk([P, T], F32, f"z{r}") for r in range(2)]
-        res = mk([P, T], F32, "res")
-        a_ps = {}
-        y_ps = {}
 
-        def copy(eng, dst, src):
-            if eng == "v":
-                nc.vector.tensor_copy(dst, src)
-            elif eng == "s":
-                nc.scalar.copy(dst, src)
-            else:
-                nc.gpsimd.tensor_scalar(dst, src, 1.0, 0.0, ALU.mult, ALU.add)
+        def quantize(words, scales, grouped):
+            nc.vector.quantize_mx(out=words.bitcast(FP8X4), scales=scales, in_=grouped)
 
-        def quantize(words, byts, src):
-            nc.vector.quantize_mx(out=words.bitcast(FP8X4), scales=byts, in_=src)
+        def product(bank, words, scales, moving_words, moving_scales):
+            nc.tensor.matmul_mx(
+                out=bank,
+                lhsT=words.bitcast(FP8X4),
+                lhsT_scale=scales,
+                rhs=moving_words.bitcast(FP8X4),
+                rhs_scale=moving_scales,
+                start=True,
+                stop=True,
+            )
 
-        def step(n):
-            if n[0] == "x":
-                a = int(n[2])
-                dst = x_grouped[a][:].rearrange("p (c i j) -> p c j i", i=4, j=4)
-                src = x_raw[:, :, 256 * a : 256 * a + 256].rearrange("p j (c i) -> p c j i", i=4)
-                r = slice(0, XV[a]) if n[1] == "v" else slice(XV[a], 64)
-                copy(n[1], dst[:, r], src[:, r])
-            elif n.startswith("qx"):
-                a = int(n[2])
-                r = slice(256 * a, 256 * a + 256)
-                quantize(x_words[:, r], x_bytes[:, r], x_grouped[a][:])
-            elif n[0] == "g":
-                k = int(n[2])
-                o = offs_sb[:, CUTS[k][0] : CUTS[k][1]]
-                if n[1] == "w":
-                    nc.vector.tensor_copy(g_words[k][:], x_words[:].indirect(o))
-                else:
-                    nc.vector.tensor_copy(g_bytes[k][:], x_bytes[:].indirect(o))
-            elif n.startswith("i2"):
-                e = int(n[2])
-                dst = w2_grouped[:, e * 512 : e * 512 + 512]
-                if W2ENG[e] == "G":
-                    copy("g", dst.rearrange("p (c j) -> p c j", j=4), w2_raw[:, e].rearrange("p j c -> p c j"))
-                else:
-                    copy(
-                        {"V": "v", "S": "s"}[W2ENG[e]],
-                        dst.rearrange("p (c i j) -> p c j i", i=4, j=4),
-                        w2_raw[:, e].rearrange("p j (c i) -> p c j i", i=4),
-                    )
-            elif n[0] == "i":
-                e = int(n[2])
-                dst = w1_grouped[e][:].rearrange("p (t m j) -> p m j t", t=4, j=4)
-                src = w1_raw[e][:].rearrange("p j (m t) -> p m j t", t=4)
-                r = {"v": slice(0, W1V[e]), "g": slice(W1V[e], W1V[e] + W1G[e]), "s": slice(W1V[e] + W1G[e], P)}[n[1]]
-                if n[1] == "g":
-                    dst = w1_grouped[e][:].rearrange("p (t m j) -> p t m j", t=4, j=4)
-                    src = w1_raw[e][:].rearrange("p j (m t) -> p t m j", t=4)
-                    for t in range(4):
-                        copy("g", dst[:, t, r], src[:, t, r])
-                else:
-                    copy(n[1], dst[:, r], src[:, r])
-            elif n.startswith("q1"):
-                e = int(n[2])
-                quantize(w1_words[e][:], w1_bytes[e][:], w1_grouped[e][:])
-            elif n.startswith("q2"):
-                e = int(n[2])
-                f = 4 if (e == 2 or Q2 == 1) else 2
-                quantize(w2_words[:, e * N : f * N], w2_bytes[:, e * N : f * N], w2_grouped[:, e * 512 : f * 512])
-            elif n.startswith("mm"):
-                e, u = int(n[2]), int(n[3])
-                bank = banks.tile([P, 4, UNIT], F32, name="a_ps")
-                a_ps[e, u] = bank
-                col = e * 16 + u * 8
-                for k, ab in enumerate(CUTS):
-                    if ab[0] <= col < ab[1]:
-                        s = slice((col - ab[0]) * 16, (col - ab[0]) * 16 + UNIT)
-                        for t in range(4):
-                            m = slice(t * P, (t + 1) * P)
-                            nc.tensor.matmul_mx(
-                                out=bank[:, t, :],
-                                lhsT=w1_words[e][:, m].bitcast(FP8X4), lhsT_scale=w1_bytes[e][:, m],
-                                rhs=g_words[k][:, s].bitcast(FP8X4), rhs_scale=g_bytes[k][:, s],
-                                start=True, stop=True,
-                            )
-            elif n.startswith("silu"):
-                e, u = int(n[4]), int(n[5])
-                nc.scalar.activation(h_grouped[e][:, u], a_ps[e, u][:].rearrange("p t n -> p n t"), ACT.Silu)
-            elif n.startswith("qh"):
-                e, u = int(n[2]), int(n[3])
-                r = slice(u * UNIT, (u + 1) * UNIT) if HQ[e] == 2 else slice(0, 2 * UNIT)
-                g = h_grouped[e][:].rearrange("p u n t -> p (u n t)")
-                quantize(h_words[e][:, r], h_bytes[e][:, r], g[:, r.start * 4 : r.stop * 4])
-            elif n.startswith("yc"):
-                e = int(n[2])
-                if YC[e][1] == 1:
-                    copy("v" if YC[e][0] == "V" else "s", y_all[:, e * C : e * C + C], y_ps[e][:])
-                else:
-                    u = int(n[3])
-                    g = YC[e][0][u] if len(YC[e][0]) == 2 else YC[e][0]
-                    copy("v" if g == "V" else "s", y_all[:, e * C + u * UNIT : e * C + (u + 1) * UNIT], y_ps[e][:, u * UNIT : (u + 1) * UNIT])
-            elif n[0] == "y":
-                e, u = int(n[1]), int(n[2])
-                if e not in y_ps:
-                    bank = banks.tile([P, 2 * UNIT], F32, name="y_ps")
-                    y_ps[e] = bank
-                r = slice(u * UNIT, (u + 1) * UNIT) if HQ[e] == 2 else slice(0, 2 * UNIT)
-                w = slice(e * N, (e + 1) * N)
-                nc.tensor.matmul_mx(
-                    out=y_ps[e][:, r],
-                    lhsT=w2_words[:, w].bitcast(FP8X4), lhsT_scale=w2_bytes[:, w],
-                    rhs=h_words[e][:, r].bitcast(FP8X4), rhs_scale=h_bytes[e][:, r],
-                    start=True, stop=True,
+        def tokens(a):
+            grouped = x_grouped[a][:].rearrange("p (g i j) -> p g j i", i=4, j=PACK)
+            raw = x_raw[a][:].rearrange("p j (g i) -> p g j i", i=4)
+            v = slice(0, X_VECTOR_GROUPS)
+            s = slice(X_VECTOR_GROUPS, HALF_T // 4)
+            nc.vector.tensor_copy(grouped[:, v], raw[:, v])
+            nc.scalar.copy(grouped[:, s], raw[:, s])
+            cols = slice(a * HALF_T, (a + 1) * HALF_T)
+            quantize(x_words[:, cols], x_bytes[:, cols], x_grouped[a][:])
+
+        def gather(k, sort):
+            lo, hi = GATHERS[k]
+            window, target = (x_words, g_words[k]) if sort == "words" else (x_bytes, g_bytes[k])
+            nc.vector.tensor_copy(target[:], window[:].indirect(offs_sb[:, lo // LANE : hi // LANE]))
+
+        def interleave_w1(e):
+            grouped = w1_grouped[e][:].rearrange("p (t m j) -> p m j t", t=PACK, j=PACK)
+            raw = w1_raw[e][:].rearrange("p j (m t) -> p m j t", t=PACK)
+            cut = W1_VECTOR_COLUMNS[e]
+            if cut > 0:
+                nc.vector.tensor_copy(grouped[:, :cut], raw[:, :cut])
+            nc.scalar.copy(grouped[:, cut:], raw[:, cut:])
+
+        def quantize_w1(e):
+            quantize(w1_words[e][:], w1_bytes[e][:], w1_grouped[e][:])
+
+        def interleave_w2(b):
+            nc.vector.tensor_copy(
+                w2_grouped[b][:].rearrange("p (e g i j) -> p e g j i", e=2, i=4, j=PACK),
+                w2_raw[b][:].rearrange("p e j (g i) -> p e g j i", i=4),
+            )
+
+        def quantize_w2(b):
+            quantize(w2_words[b][:], w2_bytes[b][:], w2_grouped[b][:])
+
+        def first_layer(e):
+            for u in range(UNITS):
+                slot = e * C + u * UNIT
+                k = [lo <= slot < hi for lo, hi in GATHERS].index(True)
+                at = slice(slot - GATHERS[k][0], slot - GATHERS[k][0] + UNIT)
+                a_bank = banks.tile([P, PACK, UNIT], F32, name="a_bank")
+                for t in range(PACK):
+                    block = slice(t * P, (t + 1) * P)
+                    product(a_bank[:, t, :], w1_words[e][:, block], w1_bytes[e][:, block], g_words[k][:, at], g_bytes[k][:, at])
+                nc.scalar.activation(
+                    h_grouped[e][:, u * UNIT : (u + 1) * UNIT, :], a_bank[:].rearrange("p t n -> p n t"), ACT.Silu
                 )
-            elif n == "z0":
-                nc.vector.tensor_tensor(z[0][:], y_all[:].indirect(pos1_sb[:]), gate_sb[:, 0, :], ALU.mult)
-            elif n[0] == "z":
-                a = 0 if n == "z1a" else 1
-                r = slice(a * 256, (a + 1) * 256)
-                nc.vector.tensor_tensor(z[1][:, r], y_all[:].indirect(pos2_sb[:, 16 * a : 16 * a + 16]), gate_sb[:, 1, r], ALU.mult)
-            else:
-                a = 0 if n == "adda" else 1
-                r = slice(a * 256, (a + 1) * 256)
-                nc.vector.tensor_tensor(res[:, r], z[0][:, r], z[1][:, r], ALU.add)
-                (nc.sync, nc.scalar)[a].dma_start(out[:, r], res[:, r])
 
-        for n in STEPS.split(" "):
-            step(n)
+        def quantize_h(e, lo, hi):
+            grouped = h_grouped[e][:].rearrange("p n t -> p (n t)")
+            quantize(h_words[e][:, lo:hi], h_bytes[e][:, lo:hi], grouped[:, lo * PACK : hi * PACK])
+
+        def second_layer(y_bank, e, lo, hi):
+            b, block = e // 2, slice((e % 2) * N, (e % 2 + 1) * N)
+            product(y_bank, w2_words[b][:, block], w2_bytes[b][:, block], h_words[e][:, lo:hi], h_bytes[e][:, lo:hi])
+
+        tokens(0)
+        tokens(1)
+        gather(0, "words")
+        gather(0, "bytes")
+        gather(1, "words")
+        gather(1, "bytes")
+        interleave_w1(0)
+        quantize_w1(0)
+        gather(2, "words")
+        interleave_w1(1)
+        interleave_w1(2)
+        first_layer(0)
+        quantize_w1(1)
+        quantize_w1(2)
+        first_layer(1)
+        interleave_w1(3)
+        quantize_h(0, 0, C)
+        gather(2, "bytes")
+        first_layer(2)
+        quantize_w1(3)
+        interleave_w2(0)
+        quantize_h(1, 0, C)
+        first_layer(3)
+        quantize_w2(0)
+        interleave_w2(1)
+
+        y01_bank = banks.tile([P, 2 * C], F32, name="y_bank")
+        second_layer(y01_bank[:, 0:C], 0, 0, C)
+        second_layer(y01_bank[:, C : 2 * C], 1, 0, C)
+        quantize_h(2, 0, C)
+        quantize_w2(1)
+        nc.scalar.copy(y_all[:, 0 : 2 * C], y01_bank[:])
+        y2_bank = banks.tile([P, C], F32, name="y_bank")
+        second_layer(y2_bank[:], 2, 0, C)
+        nc.scalar.copy(y_all[:, 2 * C : 3 * C], y2_bank[:])
+        for u in range(UNITS):
+            lo, hi = u * UNIT, (u + 1) * UNIT
+            quantize_h(3, lo, hi)
+            y3_bank = banks.tile([P, UNIT], F32, name="y_bank")
+            second_layer(y3_bank[:], 3, lo, hi)
+            nc.vector.tensor_copy(y_all[:, 3 * C + lo : 3 * C + hi], y3_bank[:])
+
+        nc.vector.tensor_tensor(z[0][:], y_all[:].indirect(pos1_sb[:]), gate_sb[:, 0, :], MULT)
+        for a, queue in enumerate((nc.sync, nc.scalar)):
+            cols = slice(a * HALF_T, (a + 1) * HALF_T)
+            entries = slice(a * HALF_T // LANE, (a + 1) * HALF_T // LANE)
+            nc.vector.tensor_tensor(z[1][:, cols], y_all[:].indirect(pos2_sb[:, entries]), gate_sb[:, 1, cols], MULT)
+            nc.vector.tensor_tensor(total[:, cols], z[0][:, cols], z[1][:, cols], ADD)
+            queue.dma_start(out[:, cols], total[:, cols])

@@ -23,7 +23,7 @@ LANE = 16
 
 GATHERS = ((0, 384), (384, 768), (768, 1024))
 X_VECTOR_GROUPS = 48
-W1_VECTOR_COLUMNS = (0, 0, 96, 96)
+W1_VECTOR_COLUMNS = (0, 0, 128, 96)
 
 
 def tile_routed_moe_kernel(tc, xT, w1, w2, gate, offs, pos1, pos2, out):
@@ -45,7 +45,7 @@ def tile_routed_moe_kernel(tc, xT, w1, w2, gate, offs, pos1, pos2, out):
         pos2_sb = lists.tile([P, T // LANE], U16, name="pos2_sb")
         x_raw = [tile([P, PACK, HALF_T], F32, f"x_raw{a}") for a in range(2)]
         w1_raw = [tile([P, PACK, H], F32, f"w1_raw{e}") for e in range(E)]
-        w2_raw = [tile([P, 2, PACK, N], F32, f"w2_raw{b}") for b in range(2)]
+        w2_raw = tile([P, E, PACK, N], F32, "w2_raw")
         gate_sb = tile([P, 2, T], F32, "gate_sb")
 
         x_rows = xT.rearrange("(p j) t -> p j t", j=PACK)
@@ -56,8 +56,7 @@ def tile_routed_moe_kernel(tc, xT, w1, w2, gate, offs, pos1, pos2, out):
             nc.sync.dma_start(x_raw[a][:], x_rows[:, :, a * HALF_T : (a + 1) * HALF_T])
         for e in range(E):
             nc.sync.dma_start(w1_raw[e][:], w1_rows[e])
-        for b in range(2):
-            nc.sync.dma_start(w2_raw[b][:], w2_rows[:, 2 * b : 2 * b + 2])
+        nc.sync.dma_start(w2_raw[:], w2_rows)
         nc.sync.dma_start(pos1_sb[:], pos1)
         nc.sync.dma_start(pos2_sb[:], pos2)
         nc.sync.dma_start(gate_sb[:], gate.rearrange("g p t -> p g t"))
@@ -117,7 +116,8 @@ def tile_routed_moe_kernel(tc, xT, w1, w2, gate, offs, pos1, pos2, out):
             cut = W1_VECTOR_COLUMNS[e]
             if cut > 0:
                 nc.vector.tensor_copy(grouped[:, :cut], raw[:, :cut])
-            nc.scalar.copy(grouped[:, cut:], raw[:, cut:])
+            if cut < P:
+                nc.scalar.copy(grouped[:, cut:], raw[:, cut:])
 
         def quantize_w1(e):
             quantize(w1_words[e][:], w1_bytes[e][:], w1_grouped[e][:])
@@ -125,7 +125,7 @@ def tile_routed_moe_kernel(tc, xT, w1, w2, gate, offs, pos1, pos2, out):
         def interleave_w2(b):
             nc.vector.tensor_copy(
                 w2_grouped[b][:].rearrange("p (e g i j) -> p e g j i", e=2, i=4, j=PACK),
-                w2_raw[b][:].rearrange("p e j (g i) -> p e g j i", i=4),
+                w2_raw[:, 2 * b : 2 * b + 2].rearrange("p e j (g i) -> p e g j i", i=4),
             )
 
         def quantize_w2(b):

from contextlib import ExitStack

import concourse.mybir as mybir

K, T, E, C, H, N = 512, 512, 4, 256, 512, 128
FLOPS = 2 * E * C * (K * H + H * N)

F32 = mybir.dt.float32
BF16 = mybir.dt.bfloat16
U32 = mybir.dt.uint32
U16 = mybir.dt.uint16
U8 = mybir.dt.uint8
FP8X4 = mybir.dt.float8_e4m3fn_x4
ACT = mybir.ActivationFunctionType
MULT, ADD = mybir.AluOpType.mult, mybir.AluOpType.add

P = 128
PACK = 4
HALF_T = T // 2
UNIT = 128
UNITS = C // UNIT
LANE = 16

GATHERS = ((0, 384), (384, 768), (768, 1024))
X_VECTOR_GROUPS = 48
W1_VECTOR_COLUMNS = (0, 0, 128, 96)


def tile_routed_moe_kernel(tc, xT, w1, w2, gate, offs, pos1, pos2, out):
    nc = tc.nc
    with ExitStack() as ctx:
        lists = ctx.enter_context(tc.tile_pool(name="lists", bufs=1))
        keep = ctx.enter_context(tc.tile_pool(name="keep", bufs=1))
        banks = ctx.enter_context(tc.psum_pool(name="banks", bufs=4))

        def tile(shape, dtype, name):
            return keep.tile(shape, dtype, name=name, align_bytes=64)

        table = tile([P, 2], F32, "table")
        nc.vector.memset(table[:, 0:1], 0.0)
        nc.scalar.activation(table[:, 1:2], table[:, 0:1], ACT.Silu)

        offs_sb = lists.tile([P, E * C // LANE], U16, name="offs_sb")
        pos1_sb = lists.tile([P, T // LANE], U16, name="pos1_sb")
        pos2_sb = lists.tile([P, T // LANE], U16, name="pos2_sb")
        x_raw = [tile([P, PACK, HALF_T], F32, f"x_raw{a}") for a in range(2)]
        w1_raw = [tile([P, PACK, H], F32, f"w1_raw{e}") for e in range(E)]
        w2_raw = tile([P, E, PACK, N], F32, "w2_raw")
        gate_sb = tile([P, 2, T], F32, "gate_sb")

        x_rows = xT.rearrange("(p j) t -> p j t", j=PACK)
        w1_rows = w1.rearrange("e (p j) i -> e p j i", j=PACK)
        w2_rows = w2.rearrange("e (p j) n -> p e j n", j=PACK)
        nc.sync.dma_start(offs_sb[:], offs)
        for a in range(2):
            nc.sync.dma_start(x_raw[a][:], x_rows[:, :, a * HALF_T : (a + 1) * HALF_T])
        for e in range(E):
            nc.sync.dma_start(w1_raw[e][:], w1_rows[e])
        nc.sync.dma_start(w2_raw[:], w2_rows)
        nc.sync.dma_start(pos1_sb[:], pos1)
        nc.sync.dma_start(pos2_sb[:], pos2)
        nc.sync.dma_start(gate_sb[:], gate.rearrange("g p t -> p g t"))

        x_grouped = [tile([P, HALF_T * PACK], BF16, f"x_grouped{a}") for a in range(2)]
        x_words = tile([P, T], U32, "x_words")
        x_bytes = tile([P, T], U8, "x_bytes")
        g_words = [tile([P, hi - lo], U32, f"g_words{lo}") for lo, hi in GATHERS]
        g_bytes = [tile([P, hi - lo], U8, f"g_bytes{lo}") for lo, hi in GATHERS]
        w1_grouped = [tile([P, H * PACK], BF16, f"w1_grouped{e}") for e in range(E)]
        w1_words = [tile([P, H], U32, f"w1_words{e}") for e in range(E)]
        w1_bytes = [tile([P, H], U8, f"w1_bytes{e}") for e in range(E)]
        w2_grouped = [tile([P, 2 * N * PACK], BF16, f"w2_grouped{b}") for b in range(2)]
        w2_words = [tile([P, 2 * N], U32, f"w2_words{b}") for b in range(2)]
        w2_bytes = [tile([P, 2 * N], U8, f"w2_bytes{b}") for b in range(2)]
        h_grouped = [tile([P, C, PACK], BF16, f"h_grouped{e}") for e in range(E)]
        h_words = [tile([P, C], U32, f"h_words{e}") for e in range(E)]
        h_bytes = [tile([P, C], U8, f"h_bytes{e}") for e in range(E)]
        y_all = tile([P, E * C], F32, "y_all")
        z = [tile([P, T], F32, f"z{r}") for r in range(2)]
        total = tile([P, T], F32, "total")

        nc.gpsimd.memset(x_bytes[:], 0)

        def quantize(words, scales, grouped):
            nc.vector.quantize_mx(out=words.bitcast(FP8X4), scales=scales, in_=grouped)

        def product(bank, words, scales, moving_words, moving_scales):
            nc.tensor.matmul_mx(
                out=bank,
                lhsT=words.bitcast(FP8X4),
                lhsT_scale=scales,
                rhs=moving_words.bitcast(FP8X4),
                rhs_scale=moving_scales,
                start=True,
                stop=True,
            )

        def tokens(a):
            grouped = x_grouped[a][:].rearrange("p (g i j) -> p g j i", i=4, j=PACK)
            raw = x_raw[a][:].rearrange("p j (g i) -> p g j i", i=4)
            v = slice(0, X_VECTOR_GROUPS)
            s = slice(X_VECTOR_GROUPS, HALF_T // 4)
            nc.vector.tensor_copy(grouped[:, v], raw[:, v])
            nc.scalar.copy(grouped[:, s], raw[:, s])
            cols = slice(a * HALF_T, (a + 1) * HALF_T)
            quantize(x_words[:, cols], x_bytes[:, cols], x_grouped[a][:])

        def gather(k, sort):
            lo, hi = GATHERS[k]
            window, target = (x_words, g_words[k]) if sort == "words" else (x_bytes, g_bytes[k])
            nc.vector.tensor_copy(target[:], window[:].indirect(offs_sb[:, lo // LANE : hi // LANE]))

        def interleave_w1(e):
            grouped = w1_grouped[e][:].rearrange("p (t m j) -> p m j t", t=PACK, j=PACK)
            raw = w1_raw[e][:].rearrange("p j (m t) -> p m j t", t=PACK)
            cut = W1_VECTOR_COLUMNS[e]
            if cut > 0:
                nc.vector.tensor_copy(grouped[:, :cut], raw[:, :cut])
            if cut < P:
                nc.scalar.copy(grouped[:, cut:], raw[:, cut:])

        def quantize_w1(e):
            quantize(w1_words[e][:], w1_bytes[e][:], w1_grouped[e][:])

        def interleave_w2(b):
            nc.vector.tensor_copy(
                w2_grouped[b][:].rearrange("p (e g i j) -> p e g j i", e=2, i=4, j=PACK),
                w2_raw[:, 2 * b : 2 * b + 2].rearrange("p e j (g i) -> p e g j i", i=4),
            )

        def quantize_w2(b):
            quantize(w2_words[b][:], w2_bytes[b][:], w2_grouped[b][:])

        def first_layer(e):
            for u in range(UNITS):
                slot = e * C + u * UNIT
                k = [lo <= slot < hi for lo, hi in GATHERS].index(True)
                at = slice(slot - GATHERS[k][0], slot - GATHERS[k][0] + UNIT)
                a_bank = banks.tile([P, PACK, UNIT], F32, name="a_bank")
                for t in range(PACK):
                    block = slice(t * P, (t + 1) * P)
                    product(a_bank[:, t, :], w1_words[e][:, block], w1_bytes[e][:, block], g_words[k][:, at], g_bytes[k][:, at])
                nc.scalar.activation(
                    h_grouped[e][:, u * UNIT : (u + 1) * UNIT, :], a_bank[:].rearrange("p t n -> p n t"), ACT.Silu
                )

        def quantize_h(e, lo, hi):
            grouped = h_grouped[e][:].rearrange("p n t -> p (n t)")
            quantize(h_words[e][:, lo:hi], h_bytes[e][:, lo:hi], grouped[:, lo * PACK : hi * PACK])

        def second_layer(y_bank, e, lo, hi):
            b, block = e // 2, slice((e % 2) * N, (e % 2 + 1) * N)
            product(y_bank, w2_words[b][:, block], w2_bytes[b][:, block], h_words[e][:, lo:hi], h_bytes[e][:, lo:hi])

        tokens(0)
        tokens(1)
        gather(0, "words")
        gather(0, "bytes")
        gather(1, "words")
        gather(1, "bytes")
        interleave_w1(0)
        quantize_w1(0)
        gather(2, "words")
        interleave_w1(1)
        interleave_w1(2)
        first_layer(0)
        quantize_w1(1)
        quantize_w1(2)
        first_layer(1)
        interleave_w1(3)
        quantize_h(0, 0, C)
        gather(2, "bytes")
        first_layer(2)
        quantize_w1(3)
        interleave_w2(0)
        quantize_h(1, 0, C)
        first_layer(3)
        quantize_w2(0)
        interleave_w2(1)

        y01_bank = banks.tile([P, 2 * C], F32, name="y_bank")
        second_layer(y01_bank[:, 0:C], 0, 0, C)
        second_layer(y01_bank[:, C : 2 * C], 1, 0, C)
        quantize_h(2, 0, C)
        quantize_w2(1)
        nc.scalar.copy(y_all[:, 0 : 2 * C], y01_bank[:])
        y2_bank = banks.tile([P, C], F32, name="y_bank")
        second_layer(y2_bank[:], 2, 0, C)
        nc.scalar.copy(y_all[:, 2 * C : 3 * C], y2_bank[:])
        for u in range(UNITS):
            lo, hi = u * UNIT, (u + 1) * UNIT
            quantize_h(3, lo, hi)
            y3_bank = banks.tile([P, UNIT], F32, name="y_bank")
            second_layer(y3_bank[:], 3, lo, hi)
            nc.vector.tensor_copy(y_all[:, 3 * C + lo : 3 * C + hi], y3_bank[:])

        nc.vector.tensor_tensor(z[0][:], y_all[:].indirect(pos1_sb[:]), gate_sb[:, 0, :], MULT)
        for a, queue in enumerate((nc.sync, nc.scalar)):
            cols = slice(a * HALF_T, (a + 1) * HALF_T)
            entries = slice(a * HALF_T // LANE, (a + 1) * HALF_T // LANE)
            nc.vector.tensor_tensor(z[1][:, cols], y_all[:].indirect(pos2_sb[:, entries]), gate_sb[:, 1, cols], MULT)
            nc.vector.tensor_tensor(total[:, cols], z[0][:, cols], z[1][:, cols], ADD)
            queue.dma_start(out[:, cols], total[:, cols])
